import numpy as np
import ml_dtypes


def mxq(x, axis, fmt="e4m3"):
    dtype, down = {"e4m3": (ml_dtypes.float8_e4m3fn, 7), "e5m2": (ml_dtypes.float8_e5m2, 14)}[fmt]
    v = np.moveaxis(np.asarray(x, np.float32).astype(ml_dtypes.bfloat16).astype(np.float64), axis, -1)
    blocks = v.reshape(v.shape[:-1] + (-1, 32))
    amax = np.abs(blocks).max(-1, keepdims=True)
    byte = np.maximum(np.where(amax > 0, np.frexp(amax)[1] - 1 + 127, 0) - down, 1)
    scale = np.exp2(byte - 127.0)
    codes = (blocks / scale).astype(np.float32).astype(dtype).astype(np.float64)
    return np.moveaxis((codes * scale).reshape(v.shape), -1, axis)


WIDE = False


def mx_kscale(k):
    if not WIDE:
        return np.ones(k)
    levels = np.array([10, -10, 5, -5, 0])
    if k % 512:
        return np.exp2(np.random.permutation(np.resize(levels, k // 32))).repeat(32)
    a = np.empty((k // 512, 16))
    for p in range(k // 512):
        a[p, :8] = np.random.permutation(np.resize(levels, 8))
        for g in range(8):
            far = levels[np.abs(levels - a[p, g]) >= 10]
            a[p, g + 8] = far[np.random.randint(len(far))]
    return np.exp2(a.ravel()).repeat(32)


def f64(x):
    return np.asarray(x).astype(np.float64)


def striped(idx):
    return np.tile(idx.reshape(-1, 16).T, (8, 1)).astype(np.uint16)


def unstriped(offs):
    return offs[:16].T.reshape(-1).astype(np.int64)


def pack_weight(w):
    k, n = w.shape
    w = f64(np.asarray(w, np.float32).astype(ml_dtypes.bfloat16)).reshape(k // 32, 32, n)
    amax = np.abs(w).max(1)
    byte = np.clip(np.where(amax > 0, np.frexp(amax)[1] - 1 + 127 - 7, 1), 1, 254)
    scaled = (w * np.exp2(127.0 - byte)[:, None, :]).reshape(k, n).astype(np.float32)
    words = np.ascontiguousarray(scaled.reshape(k // 512, 128, 4, n).transpose(0, 1, 3, 2)).astype(ml_dtypes.float8_e4m3fn).view(np.uint8)
    return words, np.ascontiguousarray(byte.astype(np.uint8).reshape(k // 512, 16, n))


def unpack_weight(words, scales):
    g, p, n, _ = words.shape
    vals = np.ascontiguousarray(words).view(ml_dtypes.float8_e4m3fn).astype(np.float64) * np.repeat(np.exp2(scales.astype(np.float64) - 127.0), 8, axis=1)[..., None]
    return vals.transpose(0, 1, 3, 2).reshape(g * 512, n)


E2M1 = np.array([0.0, 0.5, 1.0, 1.5, 2.0, 3.0, 4.0, 6.0, -0.0, -0.5, -1.0, -1.5, -2.0, -3.0, -4.0, -6.0])


def pack_fp4(w):
    k, n = w.shape
    w = f64(np.asarray(w, np.float32).astype(ml_dtypes.bfloat16)).reshape(k // 32, 32, n)
    amax = np.abs(w).max(1)
    mant, ex = np.frexp(amax / 6.0)
    byte = np.clip(np.where(amax > 0, np.where(mant > 0.5, ex, ex - 1) + 127, 1), 1, 254)
    scaled = (w * np.exp2(127.0 - byte)[:, None, :]).reshape(k, n).astype(np.float32)
    c = np.ascontiguousarray(scaled.reshape(k // 512, 128, 4, n).transpose(0, 1, 3, 2)).astype(ml_dtypes.float4_e2m1fn).view(np.uint8) & 0xF
    words = (c[..., 0::2] | (c[..., 1::2] << 4)).reshape(k // 512, 128, 2 * n)
    return np.ascontiguousarray(words), np.ascontiguousarray(byte.astype(np.uint8).reshape(k // 512, 16, n))


def unpack_fp4(words, scales):
    g, _, n = scales.shape
    words = np.ascontiguousarray(words).reshape(g, 128, n, 2)
    nib = np.empty((g, 128, n, 4), np.uint8)
    nib[..., 0::2] = words & 0xF
    nib[..., 1::2] = words >> 4
    vals = E2M1[nib] * np.repeat(np.exp2(scales.astype(np.float64) - 127.0), 8, axis=1)[..., None]
    return vals.transpose(0, 1, 3, 2).reshape(g * 512, n)


def silu(v):
    return v / (1.0 + np.exp(-np.maximum(v, -700.0)))


K, T, H, N, J, U = 1024, 1024, 512, 128, 512, 2048


def setup_inputs():
    n = np.random.standard_normal
    s = mx_kscale(K)[:, None]
    u = mx_kscale(H)
    r = mx_kscale(J)[:, None]
    packed_xT = pack_weight(n((K, T)) * s)
    packed_w2 = pack_fp4(n((H, N)) / np.sqrt(2 * H) / u[:, None])
    return {
        "x_words": packed_xT[0],
        "x_scales": packed_xT[1],
        "aT": (n((J, U)) * r).astype(np.float32),
        "w1": (n((K, H)) / np.sqrt(K) / s * u).astype(np.float32),
        "w3": (n((J, H)) / np.sqrt(J) / r).astype(np.float32),
        "w2_words": packed_w2[0],
        "w2_scales": packed_w2[1],
        "pos1": striped(np.random.permutation(T)),
        "pos2": striped(np.random.permutation(T)),
    }


def reference(x_words, x_scales, aT, w1, w3, w2_words, w2_scales, pos1, pos2):
    xq = unpack_weight(x_words, x_scales)
    h = silu(mxq(f64(w1), 0, "e4m3").T @ xq)
    f = mxq(f64(w3), 0, "e4m3").T @ mxq(f64(aT), 0, "e4m3")
    z = h[:, unstriped(pos1)] * f[:, :T] + h[:, unstriped(pos2)] * f[:, T:2 * T]
    return unpack_fp4(w2_words, w2_scales).T @ mxq(z, 0, "e4m3")

@@ -1,0 +1,325 @@
+from contextlib import ExitStack
+
+import concourse.mybir as mybir
+from concourse.masks import make_identity
+
+K, T, H, N, J, D = 1024, 1024, 512, 128, 512, 2
+FLOPS = 2 * (K * H * T + J * H * D * T + H * N * T)
+
+F32 = mybir.dt.float32
+BF16 = mybir.dt.bfloat16
+I32 = mybir.dt.int32
+U32 = mybir.dt.uint32
+U16 = mybir.dt.uint16
+U8 = mybir.dt.uint8
+FP8X4 = mybir.dt.float8_e4m3fn_x4
+FP4X4 = mybir.dt.float4_e2m1fn_x4
+SILU = mybir.ActivationFunctionType.Silu
+MULT = mybir.AluOpType.mult
+ADD = mybir.AluOpType.add
+
+P = 128
+PACK = 4
+BANK = 512
+
+
+def tile_picked_wdime_none_l_kernel(tc, x_words, x_scales, aT, w1, w3, w2_words, w2_scales, pos1, pos2, out):
+    nc = tc.nc
+    passes = K // (P * PACK)
+
+    with ExitStack() as ctx:
+        keep = ctx.enter_context(tc.tile_pool(name="keep", bufs=1))
+        psum = ctx.enter_context(tc.psum_pool(name="psum", bufs=1))
+
+        def held(shape, dtype, name):
+            return keep.tile(shape, dtype, name=name, align_bytes=64)
+
+        x_plane = held([P, T], U8, "x_plane")
+        nc.vector.memset(x_plane[:].bitcast(I32), 0)
+        w2_plane = held([P, N], U8, "w2_plane")
+        nc.vector.memset(w2_plane[:].bitcast(I32), 0)
+        warm = held([P, 2], F32, "warm")
+        nc.vector.memset(warm[:], 0.0)
+        warm_out = held([P, 2], F32, "warm_out")
+        nc.scalar.activation(warm_out[:], warm[:], SILU)
+
+        def load_weight(rows, name):
+            raw = held([P, PACK, H], F32, name)
+            nc.sync.dma_start(out=raw[:], in_=rows.rearrange("(p j) c -> p j c", j=PACK))
+            return raw
+
+        def quantise_weight(raw, name):
+            grouped = held([P, PACK, P, PACK], BF16, name + "_bf")
+            dst = grouped[:].rearrange("p t m j -> p m j t")
+            src = raw[:].rearrange("p j (m t) -> p m j t", t=PACK)
+            nc.vector.tensor_copy(out=dst[:, :84], in_=src[:, :84])
+            nc.scalar.copy(out=dst[:, 84:], in_=src[:, 84:])
+            codes = held([P, H], U32, name + "_codes")
+            plane = held([P, H], U8, name + "_plane")
+            nc.vector.quantize_mx(out=codes[:].bitcast(FP8X4), scales=plane[:], in_=grouped[:].rearrange("p t m j -> p (t m j)"))
+            return codes, plane
+
+        angles = aT.rearrange("(p j) (d v) -> p j d v", j=PACK, d=D)
+
+        def load_angles(n):
+            v0, width, d0, nd = pieces[n]
+            raw = held([P, PACK, nd, width], F32, f"a_raw{n}")
+            if nd == D:
+                nc.sync.dma_start(out=raw[:].rearrange("p j d v -> p (j d) v"), in_=angles.rearrange("p j d v -> p (j d) v")[:, :, v0 : v0 + width])
+            else:
+                nc.sync.dma_start(out=raw[:, :, 0, :], in_=angles[:, :, d0, v0 : v0 + width])
+            return raw
+
+        ident = held([P, P], F32, "ident")
+        make_identity(nc, ident[:])
+
+        w1_raw = [load_weight(w1[0 : P * PACK, :], "w1_raw0")]
+        for q in range(4):
+            nc.sync.dma_start(
+                out=x_plane[32 * q : 32 * q + 8, :].bitcast(I32),
+                in_=x_scales[:, 4 * q : 4 * q + 4, :].bitcast(I32),
+            )
+        w1_raw.append(load_weight(w1[P * PACK : 2 * P * PACK, :], "w1_raw1"))
+        x_rows = x_words.rearrange("g p n r -> p g (n r)")
+        x_codes = []
+        for half in range(2):
+            codes = held([P, passes, BANK], U32, f"x_codes{half}")
+            nc.sync.dma_start(out=codes[:].bitcast(I32), in_=x_rows[:, :, half * BANK * PACK : (half + 1) * BANK * PACK].bitcast(I32))
+            x_codes.append(codes)
+        pieces = [(0, 256, 0, 1), (256, 256, 0, 1), (0, 512, 1, 1), (512, 512, 0, 1), (512, 256, 1, 1), (768, 256, 1, 1)]
+        a_raw = [load_angles(0)]
+        w3_raw = []
+        for half in range(2):
+            raw = held([P, PACK, H // 2], F32, f"w3_raw{half}")
+            nc.sync.dma_start(out=raw[:], in_=w3[:, half * H // 2 : (half + 1) * H // 2].rearrange("(p j) c -> p j c", j=PACK))
+            w3_raw.append(raw)
+        lists = []
+        for name, pos in (("pos1", pos1), ("pos2", pos2)):
+            offsets = keep.tile([P, T // 16], U16, name=name)
+            nc.sync.dma_start(offsets[:], pos)
+            lists.append(offsets)
+        for n in range(1, len(pieces)):
+            a_raw.append(load_angles(n))
+        w2_codes = held([P, 2 * N], U8, "w2_codes")
+        nc.sync.dma_start(out=w2_codes[:].bitcast(I32), in_=w2_words[0].bitcast(I32))
+        for q in range(4):
+            nc.sync.dma_start(
+                out=w2_plane[32 * q : 32 * q + 4, :].bitcast(I32),
+                in_=w2_scales[0, 4 * q : 4 * q + 4, :].bitcast(I32),
+            )
+
+        w1_q = [quantise_weight(w1_raw[g], f"w1_{g}") for g in range(passes)]
+
+        banks = [psum.tile([P, BANK], F32, name=f"bank{b}") for b in range(8)]
+        h = [held([P, T], F32, f"h{t}") for t in range(PACK)]
+        def hidden(t, use, halves=(0, 1)):
+            m_cols = slice(t * P, (t + 1) * P)
+            for half in halves:
+                cols = slice(half * BANK, (half + 1) * BANK)
+                acc = banks[use[half]]
+                for g in range(passes):
+                    nc.tensor.matmul_mx(
+                        out=acc[:],
+                        lhsT=w1_q[g][0][:, m_cols].bitcast(FP8X4),
+                        lhsT_scale=w1_q[g][1][:, m_cols],
+                        rhs=x_codes[half][:, g, :].bitcast(FP8X4),
+                        rhs_scale=x_plane[4 * g : P, cols],
+                        start=(g == 0),
+                        stop=(g == passes - 1),
+                    )
+                nc.scalar.activation(h[t][:, cols], acc[:], SILU)
+
+        w3_bf = held([P, PACK, P, PACK], BF16, "w3_bf")
+        w3_codes = held([P, H], U32, "w3_codes")
+        w3_plane = held([P, H], U8, "w3_plane")
+
+        def cast_w3(m0, m1, on_vector):
+            half = m0 // (P // 2)
+            src = w3_raw[half][:].rearrange("p j (m t) -> p m j t", t=PACK)[:, m0 - half * P // 2 : m1 - half * P // 2]
+            dst = w3_bf[:, :, m0:m1, :].rearrange("p t m j -> p m j t")
+            if on_vector:
+                nc.vector.tensor_copy(out=dst, in_=src)
+            else:
+                nc.scalar.copy(out=dst, in_=src)
+
+        def quantise_w3(t0, t1):
+            cols = slice(t0 * P, t1 * P)
+            nc.vector.quantize_mx(out=w3_codes[:, cols].bitcast(FP8X4), scales=w3_plane[:, cols], in_=w3_bf[:, t0:t1].rearrange("p t m j -> p (t m j)"))
+
+        GUEST = {"a2": (1, 2, 512), "a3": (2, 2, 512), "a4": (3, 0, 256), "a5": (3, 2, 256), "z0": (4, 2, 256), "z256": (5, 0, 256)}
+        steps = PACK * len(pieces)
+        guest_words = {PACK * host + t: gw * PACK // 2 for (host, t, gw) in GUEST.values()}
+        f_at, product_at, room_at, end = {}, {}, {}, 0
+        for k in range(0, steps + 2, 2):
+            f_words = pieces[(k - 2) // PACK][1] if k >= 2 else pieces[0][1]
+            room = 0
+            if k < steps:
+                n = k // PACK
+                width = pieces[n][1]
+                group = (PACK * n, PACK * n + 2) if n in (3, 5) else (k,)
+                room = max([2 * (width - f_words)] + [guest_words.get(g, 0) for g in group])
+                lap = max(min(f_words, width - room // 4), 64)
+            f_at[k - 2] = end
+            room_at[k] = end + f_words
+            f_at[k - 1] = room_at[k] + room
+            if k < steps:
+                product_at[k] = room_at[k] - lap
+                product_at[k + 1] = f_at[k - 1] + lap - width
+            end = f_at[k - 1] + f_words
+        arena = held([P, end + 2048], F32, "arena")
+
+        def rows(start, pitch, count, width):
+            return arena[:, start : start + count * pitch].rearrange("p (t c) -> p t c", t=count)[:, :, :width]
+
+        def f_rows(n, t0, count):
+            k, width = PACK * n + t0, pieces[n][1]
+            pitch = f_at[k + 1] - f_at[k] if count > 1 else width
+            return rows(f_at[k], pitch, count, width)
+
+        def product(n, t):
+            start = product_at[PACK * n + t]
+            return arena[:, start : start + pieces[n][1]]
+
+        def interleaved(name, width):
+            if name in GUEST:
+                host, t, gw = GUEST[name]
+                start = room_at[PACK * host + t]
+                return arena[:, start : start + width * PACK // 2].bitcast(BF16).rearrange("p (c j) -> p c j", j=PACK)
+            return held([P, width, PACK], BF16, name)[:]
+
+        a_bf = [interleaved(f"a{n}", pieces[n][1]).rearrange("p (d c) j -> p d c j", d=1) for n in range(len(pieces))]
+
+        def cast_angles(n, c0, c1, on_vector):
+            dst = a_bf[n][:, :, c0:c1, :].rearrange("p d (c i) j -> p d c j i", i=4)
+            src = a_raw[n][:, :, :, c0:c1].rearrange("p j d (c i) -> p d c j i", i=4)
+            if on_vector:
+                nc.vector.tensor_copy(out=dst, in_=src)
+            else:
+                nc.scalar.copy(out=dst, in_=src)
+
+        def quantise_angles(n):
+            v0, width, d0, nd = pieces[n]
+            codes = held([P, nd * width], U32, f"a_codes{n}")
+            plane = held([P, nd * width], U8, f"a_plane{n}")
+            nc.vector.quantize_mx(out=codes[:].bitcast(FP8X4), scales=plane[:], in_=a_bf[n].rearrange("p d c j -> p (d c j)"))
+            return codes, plane
+
+        def filters(n, quantised, per_bank, use):
+            v0, width, d0, nd = pieces[n]
+            codes, plane = quantised
+            for t0 in range(0, PACK, per_bank):
+                acc = banks[use[t0 // per_bank]][:, : per_bank * width].rearrange("p (t c) -> p t c", t=per_bank)
+                for t in range(t0, t0 + per_bank):
+                    m_cols = slice(t * P, (t + 1) * P)
+                    nc.tensor.matmul_mx(
+                        out=acc[:, t - t0, :],
+                        lhsT=w3_codes[:, m_cols].bitcast(FP8X4),
+                        lhsT_scale=w3_plane[:, m_cols],
+                        rhs=codes[:].bitcast(FP8X4),
+                        rhs_scale=plane[:],
+                        start=True,
+                        stop=True,
+                    )
+                nc.scalar.copy(out=f_rows(n, t0, per_bank), in_=acc)
+
+        def messages(n):
+            v0, width, d, nd = pieces[n]
+            for t in range(PACK):
+                window = h[t][:].indirect(lists[d][:, v0 // 16 : (v0 + width) // 16])
+                nc.vector.tensor_tensor(product(n, t), window, f_rows(n, t, 1)[:, 0, :], MULT)
+
+        def piece_of(d, v0):
+            return [n for n, (p0, pw, pd, nd) in enumerate(pieces) if pd == d and p0 <= v0 < p0 + pw][0]
+
+        def add_on_vector(v0, width, z):
+            both = []
+            for d in range(D):
+                n = piece_of(d, v0)
+                k = PACK * n
+                assert product_at[k + 2] - product_at[k + 1] == product_at[k + 1] - product_at[k] == product_at[k + 3] - product_at[k + 2]
+                view = rows(product_at[k] + v0 - pieces[n][0], product_at[k + 1] - product_at[k], PACK, width)
+                both.append(view.rearrange("p t (c i) -> p c t i", i=2))
+            nc.vector.tensor_tensor(z.rearrange("p (c i) t -> p c t i", i=2), both[0], both[1], ADD)
+
+        def turn(v0, bank):
+            turned = banks[bank][:].rearrange("v (t p) -> v t p", t=PACK)
+            for t in range(PACK):
+                for d in range(D):
+                    n = piece_of(d, v0)
+                    c0 = v0 - pieces[n][0]
+                    nc.tensor.matmul(turned[:, t, :], lhsT=product(n, t)[:, c0 : c0 + P], rhs=ident[:], start=(d == 0), stop=(d == D - 1), is_transpose=True)
+            rounded = held([P, 2, P, 2], BF16, f"rounded{v0}")
+            nc.scalar.copy(out=rounded[:], in_=turned.rearrange("v (u e) p -> v u p e", e=2))
+            return rounded
+
+        def turn_back(roundeds, bank, z):
+            back = banks[bank][:, : len(roundeds) * 2 * P].rearrange("p (b u v) -> p b u v", u=2, v=P)
+            for b, rounded in enumerate(roundeds):
+                words = rounded[:].rearrange("v u p e -> v (u p e)").bitcast(F32)
+                for u in range(2):
+                    nc.tensor.transpose(back[:, b, u, :], words[:, u * P : (u + 1) * P], ident[:])
+            z_words = z.rearrange("p c t -> p (c t)").bitcast(F32).rearrange("p (b v u) -> p b v u", u=2, v=P)
+            nc.scalar.copy(out=z_words, in_=back.rearrange("p b u v -> p b v u"))
+
+        def project(v0, width, z, bank):
+            codes = held([P, width], U32, f"z_codes{v0}")
+            plane = held([P, width], U8, f"z_plane{v0}")
+            nc.vector.quantize_mx(out=codes[:].bitcast(FP8X4), scales=plane[:], in_=z.rearrange("p c t -> p (c t)"))
+            acc = banks[bank][:, :width]
+            nc.tensor.matmul_mx(
+                out=acc[:],
+                lhsT=w2_codes[:].bitcast(FP4X4),
+                lhsT_scale=w2_plane[:],
+                rhs=codes[:].bitcast(FP8X4),
+                rhs_scale=plane[:],
+                start=True,
+                stop=True,
+            )
+            res = held([P, width], F32, f"res{v0}")
+            nc.scalar.copy(out=res[:], in_=acc[:])
+            nc.sync.dma_start(out=out[:, v0 : v0 + width], in_=res[:])
+
+        z = {v0: interleaved(f"z{v0}", width) for v0, width in ((0, 256), (256, 256), (512, 256), (768, 128), (896, 128))}
+        hidden(0, (0, 1))
+        hidden(1, (2, 3))
+        cast_angles(0, 0, 256, True)
+        q0 = quantise_angles(0)
+        cast_w3(0, 64, True)
+        cast_w3(64, 128, True)
+        quantise_w3(0, 1)
+        quantise_w3(1, 2)
+        quantise_w3(2, 4)
+        hidden(2, (0, 1))
+        hidden(3, (2, 7), (0,))
+        filters(0, q0, 1, (7, 4, 5, 6))
+        hidden(3, (6, 7), (1,))
+        cast_angles(1, 0, 256, True)
+        filters(1, quantise_angles(1), 2, (0, 1))
+        cast_angles(2, 0, 256, False)
+        messages(0)
+        cast_angles(2, 256, 512, True)
+        filters(2, quantise_angles(2), 1, (2, 3, 4, 5))
+        messages(1)
+        cast_angles(3, 0, 512, False)
+        filters(3, quantise_angles(3), 1, (6, 7, 4, 5))
+        messages(2)
+        cast_angles(4, 0, 256, False)
+        filters(4, quantise_angles(4), 2, (0, 1))
+        cast_angles(5, 0, 256, False)
+        filters(5, quantise_angles(5), 2, (2, 3))
+        r = [turn(0, 4), turn(128, 0)]
+        turn_back(r, 5, z[0])
+        messages(3)
+        r = [turn(256, 2), turn(384, 6)]
+        turn_back(r, 7, z[256])
+        project(0, 256, z[0], 1)
+        messages(4)
+        project(256, 256, z[256], 3)
+        r = [turn(512, 7), turn(640, 5)]
+        turn_back(r, 4, z[512])
+        messages(5)
+        add_on_vector(768, 128, z[768])
+        add_on_vector(896, 128, z[896])
+        project(512, 256, z[512], 0)
+        project(768, 128, z[768], 6)
+        project(896, 128, z[896], 2)

@@ -50,10 +50,10 @@ def tile_picked_wdime_none_l_kernel(tc, x_words, x_scales, aT, w1, w3, w2_words,
 
         def quantise_weight(raw, name):
             grouped = held([P, PACK, P, PACK], BF16, name + "_bf")
-            dst = grouped[:].rearrange("p t m j -> p m j t")
-            src = raw[:].rearrange("p j (m t) -> p m j t", t=PACK)
-            nc.vector.tensor_copy(out=dst[:, :84], in_=src[:, :84])
-            nc.scalar.copy(out=dst[:, 84:], in_=src[:, 84:])
+            dst = grouped[:].rearrange("p t m j -> p m t j")
+            src = raw[:].rearrange("p j (m t) -> p m t j", t=PACK)
+            nc.vector.tensor_copy(out=dst[:, :88], in_=src[:, :88])
+            nc.scalar.copy(out=dst[:, 88:], in_=src[:, 88:])
             codes = held([P, H], U32, name + "_codes")
             plane = held([P, H], U8, name + "_plane")
             nc.vector.quantize_mx(out=codes[:].bitcast(FP8X4), scales=plane[:], in_=grouped[:].rearrange("p t m j -> p (t m j)"))
@@ -79,13 +79,16 @@ def tile_picked_wdime_none_l_kernel(tc, x_words, x_scales, aT, w1, w3, w2_words,
                 out=x_plane[32 * q : 32 * q + 8, :].bitcast(I32),
                 in_=x_scales[:, 4 * q : 4 * q + 4, :].bitcast(I32),
             )
-        w1_raw.append(load_weight(w1[P * PACK : 2 * P * PACK, :], "w1_raw1"))
-        x_rows = x_words.rearrange("g p n r -> p g (n r)")
         x_codes = []
-        for half in range(2):
-            codes = held([P, passes, BANK], U32, f"x_codes{half}")
-            nc.sync.dma_start(out=codes[:].bitcast(I32), in_=x_rows[:, :, half * BANK * PACK : (half + 1) * BANK * PACK].bitcast(I32))
+
+        def load_x(g):
+            codes = held([P, T], U32, f"x_codes{g}")
+            nc.sync.dma_start(out=codes[:].bitcast(I32), in_=x_words[g].rearrange("p n r -> p (n r)").bitcast(I32))
             x_codes.append(codes)
+
+        w1_raw.append(load_weight(w1[P * PACK : 2 * P * PACK, :], "w1_raw1"))
+        load_x(0)
+        load_x(1)
         pieces = [(0, 256, 0, 1), (256, 256, 0, 1), (0, 512, 1, 1), (512, 512, 0, 1), (512, 256, 1, 1), (768, 256, 1, 1)]
         a_raw = [load_angles(0)]
         w3_raw = []
@@ -94,12 +97,17 @@ def tile_picked_wdime_none_l_kernel(tc, x_words, x_scales, aT, w1, w3, w2_words,
             nc.sync.dma_start(out=raw[:], in_=w3[:, half * H // 2 : (half + 1) * H // 2].rearrange("(p j) c -> p j c", j=PACK))
             w3_raw.append(raw)
         lists = []
-        for name, pos in (("pos1", pos1), ("pos2", pos2)):
+
+        def load_list(name, pos):
             offsets = keep.tile([P, T // 16], U16, name=name)
             nc.sync.dma_start(offsets[:], pos)
             lists.append(offsets)
+
+        load_list("pos1", pos1)
         for n in range(1, len(pieces)):
             a_raw.append(load_angles(n))
+            if n == 2:
+                load_list("pos2", pos2)
         w2_codes = held([P, 2 * N], U8, "w2_codes")
         nc.sync.dma_start(out=w2_codes[:].bitcast(I32), in_=w2_words[0].bitcast(I32))
         for q in range(4):
@@ -122,7 +130,7 @@ def tile_picked_wdime_none_l_kernel(tc, x_words, x_scales, aT, w1, w3, w2_words,
                         out=acc[:],
                         lhsT=w1_q[g][0][:, m_cols].bitcast(FP8X4),
                         lhsT_scale=w1_q[g][1][:, m_cols],
-                        rhs=x_codes[half][:, g, :].bitcast(FP8X4),
+                        rhs=x_codes[g][:, cols].bitcast(FP8X4),
                         rhs_scale=x_plane[4 * g : P, cols],
                         start=(g == 0),
                         stop=(g == passes - 1),
@@ -135,8 +143,8 @@ def tile_picked_wdime_none_l_kernel(tc, x_words, x_scales, aT, w1, w3, w2_words,
 
         def cast_w3(m0, m1, on_vector):
             half = m0 // (P // 2)
-            src = w3_raw[half][:].rearrange("p j (m t) -> p m j t", t=PACK)[:, m0 - half * P // 2 : m1 - half * P // 2]
-            dst = w3_bf[:, :, m0:m1, :].rearrange("p t m j -> p m j t")
+            src = w3_raw[half][:].rearrange("p j (m t) -> p m t j", t=PACK)[:, m0 - half * P // 2 : m1 - half * P // 2]
+            dst = w3_bf[:, :, m0:m1, :].rearrange("p t m j -> p m t j")
             if on_vector:
                 nc.vector.tensor_copy(out=dst, in_=src)
             else:
@@ -279,7 +287,8 @@ def tile_picked_wdime_none_l_kernel(tc, x_words, x_scales, aT, w1, w3, w2_words,
             nc.scalar.copy(out=res[:], in_=acc[:])
             nc.sync.dma_start(out=out[:, v0 : v0 + width], in_=res[:])
 
-        z = {v0: interleaved(f"z{v0}", width) for v0, width in ((0, 256), (256, 256), (512, 256), (768, 128), (896, 128))}
+        z = {v0: interleaved(f"z{v0}", width) for v0, width in ((0, 256), (256, 256), (512, 256), (896, 128))}
+        z[768] = z[512][:, :128, :]
         hidden(0, (0, 1))
         hidden(1, (2, 3))
         cast_angles(0, 0, 256, True)
@@ -314,12 +323,12 @@ def tile_picked_wdime_none_l_kernel(tc, x_words, x_scales, aT, w1, w3, w2_words,
         turn_back(r, 7, z[256])
         project(0, 256, z[0], 1)
         messages(4)
-        project(256, 256, z[256], 3)
         r = [turn(512, 7), turn(640, 5)]
+        project(256, 256, z[256], 7)
         turn_back(r, 4, z[512])
         messages(5)
+        project(512, 256, z[512], 0)
         add_on_vector(768, 128, z[768])
         add_on_vector(896, 128, z[896])
-        project(512, 256, z[512], 0)
         project(768, 128, z[768], 6)
         project(896, 128, z[896], 2)

@@ -63,7 +63,11 @@ def tile_picked_wdime_none_l_kernel(tc, x_words, x_scales, aT, w1, w3, w2_words,
 
         def load_angles(n):
             v0, width, d0, nd = pieces[n]
-            raw = held([P, PACK, nd, width], F32, f"a_raw{n}")
+            if n in RAW_ON:
+                start = f_at[RAW_ON[n]] + width // 2
+                raw = arena[:, start : start + PACK * width].rearrange("p (j d c) -> p j d c", j=PACK, d=1)
+            else:
+                raw = held([P, PACK, nd, width], F32, f"a_raw{n}")[:]
             if nd == D:
                 nc.sync.dma_start(out=raw[:].rearrange("p j d v -> p (j d) v"), in_=angles.rearrange("p j d v -> p (j d) v")[:, :, v0 : v0 + width])
             else:
@@ -73,23 +77,43 @@ def tile_picked_wdime_none_l_kernel(tc, x_words, x_scales, aT, w1, w3, w2_words,
         ident = held([P, P], F32, "ident")
         make_identity(nc, ident[:])
 
+        pieces = [(0, 256, 0, 1), (256, 256, 0, 1), (0, 512, 1, 1), (512, 512, 0, 1), (512, 256, 1, 1), (768, 256, 1, 1)]
+        RAW_ON = {3: 8}
+        GUEST = {"a1": (0, 2, 256), "a2": (1, 2, 512), "a3": (2, 0, 512), "a4": (3, 0, 256), "a5": (3, 2, 256), "z0": (4, 2, 256), "z256": (5, 0, 256)}
+        steps = PACK * len(pieces)
+        guest_words = {PACK * host + t: gw * PACK // 2 for (host, t, gw) in GUEST.values()}
+        f_at, product_at, room_at, end = {}, {}, {}, 0
+        for k in range(0, steps + 2, 2):
+            f_words = pieces[(k - 2) // PACK][1] if k >= 2 else pieces[0][1]
+            room = 0
+            if k < steps:
+                n = k // PACK
+                width = pieces[n][1]
+                group = (PACK * n, PACK * n + 2) if n in (3, 5) else (k,)
+                room = max([2 * (width - f_words)] + [guest_words.get(g, 0) for g in group])
+                lap = max(min(f_words, width - room // 4), 64)
+            f_at[k - 2] = end
+            room_at[k] = end + f_words
+            f_at[k - 1] = room_at[k] + room
+            if k < steps:
+                product_at[k] = room_at[k] - lap
+                product_at[k + 1] = f_at[k - 1] + lap - width
+            end = f_at[k - 1] + f_words
+        arena = held([P, end + 2048], F32, "arena")
+
         w1_raw = [load_weight(w1[0 : P * PACK, :], "w1_raw0")]
         for q in range(4):
             nc.sync.dma_start(
                 out=x_plane[32 * q : 32 * q + 8, :].bitcast(I32),
                 in_=x_scales[:, 4 * q : 4 * q + 4, :].bitcast(I32),
             )
-        x_codes = []
-
-        def load_x(g):
-            codes = held([P, T], U32, f"x_codes{g}")
-            nc.sync.dma_start(out=codes[:].bitcast(I32), in_=x_words[g].rearrange("p n r -> p (n r)").bitcast(I32))
-            x_codes.append(codes)
-
         w1_raw.append(load_weight(w1[P * PACK : 2 * P * PACK, :], "w1_raw1"))
-        load_x(0)
-        load_x(1)
-        pieces = [(0, 256, 0, 1), (256, 256, 0, 1), (0, 512, 1, 1), (512, 512, 0, 1), (512, 256, 1, 1), (768, 256, 1, 1)]
+        x_rows = x_words.rearrange("g p n r -> p g (n r)")
+        x_codes = []
+        for half in range(2):
+            codes = held([P, passes, BANK], U32, f"x_codes{half}")
+            nc.sync.dma_start(out=codes[:].bitcast(I32), in_=x_rows[:, :, half * BANK * PACK : (half + 1) * BANK * PACK].bitcast(I32))
+            x_codes.append(codes)
         a_raw = [load_angles(0)]
         w3_raw = []
         for half in range(2):
@@ -130,7 +154,7 @@ def tile_picked_wdime_none_l_kernel(tc, x_words, x_scales, aT, w1, w3, w2_words,
                         out=acc[:],
                         lhsT=w1_q[g][0][:, m_cols].bitcast(FP8X4),
                         lhsT_scale=w1_q[g][1][:, m_cols],
-                        rhs=x_codes[g][:, cols].bitcast(FP8X4),
+                        rhs=x_codes[half][:, g, :].bitcast(FP8X4),
                         rhs_scale=x_plane[4 * g : P, cols],
                         start=(g == 0),
                         stop=(g == passes - 1),
@@ -153,28 +177,6 @@ def tile_picked_wdime_none_l_kernel(tc, x_words, x_scales, aT, w1, w3, w2_words,
         def quantise_w3(t0, t1):
             cols = slice(t0 * P, t1 * P)
             nc.vector.quantize_mx(out=w3_codes[:, cols].bitcast(FP8X4), scales=w3_plane[:, cols], in_=w3_bf[:, t0:t1].rearrange("p t m j -> p (t m j)"))
-
-        GUEST = {"a2": (1, 2, 512), "a3": (2, 2, 512), "a4": (3, 0, 256), "a5": (3, 2, 256), "z0": (4, 2, 256), "z256": (5, 0, 256)}
-        steps = PACK * len(pieces)
-        guest_words = {PACK * host + t: gw * PACK // 2 for (host, t, gw) in GUEST.values()}
-        f_at, product_at, room_at, end = {}, {}, {}, 0
-        for k in range(0, steps + 2, 2):
-            f_words = pieces[(k - 2) // PACK][1] if k >= 2 else pieces[0][1]
-            room = 0
-            if k < steps:
-                n = k // PACK
-                width = pieces[n][1]
-                group = (PACK * n, PACK * n + 2) if n in (3, 5) else (k,)
-                room = max([2 * (width - f_words)] + [guest_words.get(g, 0) for g in group])
-                lap = max(min(f_words, width - room // 4), 64)
-            f_at[k - 2] = end
-            room_at[k] = end + f_words
-            f_at[k - 1] = room_at[k] + room
-            if k < steps:
-                product_at[k] = room_at[k] - lap
-                product_at[k + 1] = f_at[k - 1] + lap - width
-            end = f_at[k - 1] + f_words
-        arena = held([P, end + 2048], F32, "arena")
 
         def rows(start, pitch, count, width):
             return arena[:, start : start + count * pitch].rearrange("p (t c) -> p t c", t=count)[:, :, :width]
@@ -249,16 +251,23 @@ def tile_picked_wdime_none_l_kernel(tc, x_words, x_scales, aT, w1, w3, w2_words,
                 both.append(view.rearrange("p t (c i) -> p c t i", i=2))
             nc.vector.tensor_tensor(z.rearrange("p (c i) t -> p c t i", i=2), both[0], both[1], ADD)
 
-        def turn(v0, bank):
-            turned = banks[bank][:].rearrange("v (t p) -> v t p", t=PACK)
+        def turn(blocks):
             for t in range(PACK):
-                for d in range(D):
-                    n = piece_of(d, v0)
-                    c0 = v0 - pieces[n][0]
-                    nc.tensor.matmul(turned[:, t, :], lhsT=product(n, t)[:, c0 : c0 + P], rhs=ident[:], start=(d == 0), stop=(d == D - 1), is_transpose=True)
+                for v0, bank in blocks:
+                    for d in reversed(range(D)):
+                        n = piece_of(d, v0)
+                        c0 = v0 - pieces[n][0]
+                        nc.tensor.matmul(banks[bank][:, t * P : (t + 1) * P], lhsT=product(n, t)[:, c0 : c0 + P], rhs=ident[:], start=(d == D - 1), stop=(d == 0), is_transpose=True)
+
+        def round_sums(v0, bank):
             rounded = held([P, 2, P, 2], BF16, f"rounded{v0}")
-            nc.scalar.copy(out=rounded[:], in_=turned.rearrange("v (u e) p -> v u p e", e=2))
+            nc.scalar.copy(out=rounded[:], in_=banks[bank][:].rearrange("v (u e p) -> v u p e", u=2, e=2))
             return rounded
+
+        def warm_up(bank, count):
+            codes, plane = w1_q[0]
+            for i in range(count):
+                nc.tensor.matmul_mx(out=banks[bank][:], lhsT=codes[:, :P].bitcast(FP8X4), lhsT_scale=plane[:, :P], rhs=codes[:].bitcast(FP8X4), rhs_scale=plane[:], start=True, stop=True)
 
         def turn_back(roundeds, bank, z):
             back = banks[bank][:, : len(roundeds) * 2 * P].rearrange("p (b u v) -> p b u v", u=2, v=P)
@@ -287,8 +296,10 @@ def tile_picked_wdime_none_l_kernel(tc, x_words, x_scales, aT, w1, w3, w2_words,
             nc.scalar.copy(out=res[:], in_=acc[:])
             nc.sync.dma_start(out=out[:, v0 : v0 + width], in_=res[:])
 
-        z = {v0: interleaved(f"z{v0}", width) for v0, width in ((0, 256), (256, 256), (512, 256), (896, 128))}
+        z = {v0: interleaved(f"z{v0}", width) for v0, width in ((0, 256), (256, 256), (512, 256))}
         z[768] = z[512][:, :128, :]
+        z[896] = z[512][:, 128:, :]
+        warm_up(7, 3)
         hidden(0, (0, 1))
         hidden(1, (2, 3))
         cast_angles(0, 0, 256, True)
@@ -298,37 +309,39 @@ def tile_picked_wdime_none_l_kernel(tc, x_words, x_scales, aT, w1, w3, w2_words,
         quantise_w3(0, 1)
         quantise_w3(1, 2)
         quantise_w3(2, 4)
+        filters(0, q0, 1, (4, 5, 6, 7))
         hidden(2, (0, 1))
-        hidden(3, (2, 7), (0,))
-        filters(0, q0, 1, (7, 4, 5, 6))
-        hidden(3, (6, 7), (1,))
+        hidden(3, (2, 3))
         cast_angles(1, 0, 256, True)
         filters(1, quantise_angles(1), 2, (0, 1))
         cast_angles(2, 0, 256, False)
         messages(0)
         cast_angles(2, 256, 512, True)
+        cast_angles(3, 0, 512, False)
         filters(2, quantise_angles(2), 1, (2, 3, 4, 5))
         messages(1)
-        cast_angles(3, 0, 512, False)
         filters(3, quantise_angles(3), 1, (6, 7, 4, 5))
         messages(2)
         cast_angles(4, 0, 256, False)
-        filters(4, quantise_angles(4), 2, (0, 1))
+        q4 = quantise_angles(4)
         cast_angles(5, 0, 256, False)
-        filters(5, quantise_angles(5), 2, (2, 3))
-        r = [turn(0, 4), turn(128, 0)]
-        turn_back(r, 5, z[0])
+        q5 = quantise_angles(5)
+        turn([(0, 0), (128, 1), (256, 2), (384, 3)])
+        r = [round_sums(128 * b, b) for b in range(4)]
+        filters(4, q4, 2, (6, 7))
+        turn_back(r[:2], 0, z[0])
+        turn_back(r[2:], 2, z[256])
+        filters(5, q5, 2, (4, 5))
         messages(3)
-        r = [turn(256, 2), turn(384, 6)]
-        turn_back(r, 7, z[256])
         project(0, 256, z[0], 1)
         messages(4)
-        r = [turn(512, 7), turn(640, 5)]
-        project(256, 256, z[256], 7)
-        turn_back(r, 4, z[512])
+        turn([(512, 2), (640, 3)])
+        r = [round_sums(512, 2), round_sums(640, 3)]
+        turn_back(r, 6, z[512])
+        project(256, 256, z[256], 6)
         messages(5)
-        project(512, 256, z[512], 0)
+        project(512, 256, z[512], 7)
         add_on_vector(768, 128, z[768])
         add_on_vector(896, 128, z[896])
-        project(768, 128, z[768], 6)
-        project(896, 128, z[896], 2)
+        project(768, 128, z[768], 4)
+        project(896, 128, z[896], 5)

@@ -20,12 +20,50 @@ ADD = mybir.AluOpType.add
 
 P = 128
 PACK = 4
+PASSES = K // (P * PACK)
 BANK = 512
+QUADRANT = 32
+PER_COLUMN = 16
+Z_WIDTH = 256
+WARM_PASSES = 3
+
+PIECES = [(0, 0, 256), (0, 256, 256), (1, 0, 512), (0, 512, 512), (1, 512, 256), (1, 768, 256)]
+SUMMED_ON_VECTOR = (3, 5)
+SCALAR_SHARE = 320
+
+QUANTISED_BEFORE_GATHER = {"a1": 2, "a2": 6, "a3": 8, "a4": 12, "a5": 14, "z0": 18, "z256": 20}
+MIN_LAP = 64
+
+
+def arena_layout():
+    gathers = PACK * len(PIECES)
+    guest_words = {}
+    for name, k in QUANTISED_BEFORE_GATHER.items():
+        columns = PIECES[int(name[1:])][2] if name.startswith("a") else Z_WIDTH
+        guest_words.setdefault(k, columns * PACK // 2)
+    filter_at, product_at, room_at, end = {}, {}, {}, 0
+    for k in range(0, gathers, 2):
+        n = k // PACK
+        width = PIECES[n][2]
+        old_width = PIECES[max(k - 2, 0) // PACK][2]
+        pairs = (PACK * n, PACK * n + 2) if n in SUMMED_ON_VECTOR else (k,)
+        room = max([2 * (width - old_width)] + [guest_words.get(pair, 0) for pair in pairs])
+        lap = max(min(old_width, width - room // 4), MIN_LAP)
+        filter_at[k - 2] = end
+        room_at[k] = end + old_width
+        filter_at[k - 1] = room_at[k] + room
+        product_at[k] = room_at[k] - lap
+        product_at[k + 1] = filter_at[k - 1] + lap - width
+        end = filter_at[k - 1] + old_width
+    last_width = PIECES[-1][2]
+    filter_at[gathers - 2] = end
+    filter_at[gathers - 1] = end + last_width
+    return filter_at, product_at, room_at, end + 2 * last_width
 
 
 def tile_picked_wdime_none_l_kernel(tc, x_words, x_scales, aT, w1, w3, w2_words, w2_scales, pos1, pos2, out):
     nc = tc.nc
-    passes = K // (P * PACK)
+    filter_at, product_at, room_at, arena_words = arena_layout()
 
     with ExitStack() as ctx:
         keep = ctx.enter_context(tc.tile_pool(name="keep", bufs=1))
@@ -35,313 +73,254 @@ def tile_picked_wdime_none_l_kernel(tc, x_words, x_scales, aT, w1, w3, w2_words,
             return keep.tile(shape, dtype, name=name, align_bytes=64)
 
         x_plane = held([P, T], U8, "x_plane")
-        nc.vector.memset(x_plane[:].bitcast(I32), 0)
+        nc.gpsimd.memset(x_plane[:].bitcast(I32), 0)
         w2_plane = held([P, N], U8, "w2_plane")
         nc.vector.memset(w2_plane[:].bitcast(I32), 0)
-        warm = held([P, 2], F32, "warm")
-        nc.vector.memset(warm[:], 0.0)
-        warm_out = held([P, 2], F32, "warm_out")
-        nc.scalar.activation(warm_out[:], warm[:], SILU)
-
-        def load_weight(rows, name):
-            raw = held([P, PACK, H], F32, name)
-            nc.sync.dma_start(out=raw[:], in_=rows.rearrange("(p j) c -> p j c", j=PACK))
-            return raw
-
-        def quantise_weight(raw, name):
-            grouped = held([P, PACK, P, PACK], BF16, name + "_bf")
-            dst = grouped[:].rearrange("p t m j -> p m t j")
-            src = raw[:].rearrange("p j (m t) -> p m t j", t=PACK)
-            nc.vector.tensor_copy(out=dst[:, :88], in_=src[:, :88])
-            nc.scalar.copy(out=dst[:, 88:], in_=src[:, 88:])
-            codes = held([P, H], U32, name + "_codes")
-            plane = held([P, H], U8, name + "_plane")
-            nc.vector.quantize_mx(out=codes[:].bitcast(FP8X4), scales=plane[:], in_=grouped[:].rearrange("p t m j -> p (t m j)"))
-            return codes, plane
-
-        angles = aT.rearrange("(p j) (d v) -> p j d v", j=PACK, d=D)
-
-        def load_angles(n):
-            v0, width, d0, nd = pieces[n]
-            if n in RAW_ON:
-                start = f_at[RAW_ON[n]] + width // 2
-                raw = arena[:, start : start + PACK * width].rearrange("p (j d c) -> p j d c", j=PACK, d=1)
-            else:
-                raw = held([P, PACK, nd, width], F32, f"a_raw{n}")[:]
-            if nd == D:
-                nc.sync.dma_start(out=raw[:].rearrange("p j d v -> p (j d) v"), in_=angles.rearrange("p j d v -> p (j d) v")[:, :, v0 : v0 + width])
-            else:
-                nc.sync.dma_start(out=raw[:, :, 0, :], in_=angles[:, :, d0, v0 : v0 + width])
-            return raw
-
         ident = held([P, P], F32, "ident")
         make_identity(nc, ident[:])
+        arena = held([P, arena_words], F32, "arena")
 
-        pieces = [(0, 256, 0, 1), (256, 256, 0, 1), (0, 512, 1, 1), (512, 512, 0, 1), (512, 256, 1, 1), (768, 256, 1, 1)]
-        RAW_ON = {3: 8}
-        GUEST = {"a1": (0, 2, 256), "a2": (1, 2, 512), "a3": (2, 0, 512), "a4": (3, 0, 256), "a5": (3, 2, 256), "z0": (4, 2, 256), "z256": (5, 0, 256)}
-        steps = PACK * len(pieces)
-        guest_words = {PACK * host + t: gw * PACK // 2 for (host, t, gw) in GUEST.values()}
-        f_at, product_at, room_at, end = {}, {}, {}, 0
-        for k in range(0, steps + 2, 2):
-            f_words = pieces[(k - 2) // PACK][1] if k >= 2 else pieces[0][1]
-            room = 0
-            if k < steps:
-                n = k // PACK
-                width = pieces[n][1]
-                group = (PACK * n, PACK * n + 2) if n in (3, 5) else (k,)
-                room = max([2 * (width - f_words)] + [guest_words.get(g, 0) for g in group])
-                lap = max(min(f_words, width - room // 4), 64)
-            f_at[k - 2] = end
-            room_at[k] = end + f_words
-            f_at[k - 1] = room_at[k] + room
-            if k < steps:
-                product_at[k] = room_at[k] - lap
-                product_at[k + 1] = f_at[k - 1] + lap - width
-            end = f_at[k - 1] + f_words
-        arena = held([P, end + 2048], F32, "arena")
+        def load_rows(rows, name):
+            raw = held([P, PACK, rows.shape[1]], F32, name)
+            nc.sync.dma_start(out=raw[:], in_=rows.rearrange("(p j) c -> p j c", j=PACK))
+            return raw[:]
 
-        w1_raw = [load_weight(w1[0 : P * PACK, :], "w1_raw0")]
-        for q in range(4):
-            nc.sync.dma_start(
-                out=x_plane[32 * q : 32 * q + 8, :].bitcast(I32),
-                in_=x_scales[:, 4 * q : 4 * q + 4, :].bitcast(I32),
-            )
-        w1_raw.append(load_weight(w1[P * PACK : 2 * P * PACK, :], "w1_raw1"))
-        x_rows = x_words.rearrange("g p n r -> p g (n r)")
-        x_codes = []
-        for half in range(2):
-            codes = held([P, passes, BANK], U32, f"x_codes{half}")
-            nc.sync.dma_start(out=codes[:].bitcast(I32), in_=x_rows[:, :, half * BANK * PACK : (half + 1) * BANK * PACK].bitcast(I32))
-            x_codes.append(codes)
-        a_raw = [load_angles(0)]
-        w3_raw = []
-        for half in range(2):
-            raw = held([P, PACK, H // 2], F32, f"w3_raw{half}")
-            nc.sync.dma_start(out=raw[:], in_=w3[:, half * H // 2 : (half + 1) * H // 2].rearrange("(p j) c -> p j c", j=PACK))
-            w3_raw.append(raw)
-        lists = []
+        def piece_columns(n):
+            d, v0, width = PIECES[n]
+            return aT[:, d * T + v0 : d * T + v0 + width]
+
+        def load_x_scales(g):
+            by_row = x_scales[g].rearrange("(q r) c -> r q c", r=4)
+            for r in range(4):
+                nc.sync.dma_start(out=x_plane[4 * g + r : P : QUADRANT, :].bitcast(I32), in_=by_row[r].bitcast(I32))
+
+        def load_x_codes(half):
+            codes = held([P, PASSES, BANK], U32, f"x_codes{half}")
+            byte_rows = x_words.rearrange("g p n r -> p g (n r)")
+            nc.sync.dma_start(out=codes[:].bitcast(I32), in_=byte_rows[:, :, half * BANK * PACK : (half + 1) * BANK * PACK].bitcast(I32))
+            return codes
 
         def load_list(name, pos):
-            offsets = keep.tile([P, T // 16], U16, name=name)
+            offsets = keep.tile([P, T // PER_COLUMN], U16, name=name)
             nc.sync.dma_start(offsets[:], pos)
-            lists.append(offsets)
+            return offsets
 
-        load_list("pos1", pos1)
-        for n in range(1, len(pieces)):
-            a_raw.append(load_angles(n))
-            if n == 2:
-                load_list("pos2", pos2)
+        w1_raw = [load_rows(w1[: P * PACK, :], "w1_raw0")]
+        load_x_scales(0)
+        w1_raw.append(load_rows(w1[P * PACK :, :], "w1_raw1"))
+        x_codes = [load_x_codes(0)]
+        load_x_scales(1)
+        x_codes.append(load_x_codes(1))
+        a_raw = [load_rows(piece_columns(0), "a_raw0")]
+        w3_raw = [load_rows(w3[:, half * H // 2 : (half + 1) * H // 2], f"w3_raw{half}") for half in range(2)]
+        lists = [load_list("pos1", pos1)]
+        a_raw.extend(load_rows(piece_columns(n), f"a_raw{n}") for n in (1, 2))
+        lists.append(load_list("pos2", pos2))
+        raw_at = filter_at[PACK * 2] + PIECES[2][2] // 2
+        piece3_raw = arena[:, raw_at : raw_at + PACK * PIECES[3][2]].rearrange("p (j c) -> p j c", j=PACK)
+        nc.sync.dma_start(out=piece3_raw, in_=piece_columns(3).rearrange("(p j) c -> p j c", j=PACK))
+        a_raw.append(piece3_raw)
+        a_raw.extend(load_rows(piece_columns(n), f"a_raw{n}") for n in (4, 5))
         w2_codes = held([P, 2 * N], U8, "w2_codes")
         nc.sync.dma_start(out=w2_codes[:].bitcast(I32), in_=w2_words[0].bitcast(I32))
         for q in range(4):
             nc.sync.dma_start(
-                out=w2_plane[32 * q : 32 * q + 4, :].bitcast(I32),
+                out=w2_plane[QUADRANT * q : QUADRANT * q + 4, :].bitcast(I32),
                 in_=w2_scales[0, 4 * q : 4 * q + 4, :].bitcast(I32),
             )
 
-        w1_q = [quantise_weight(w1_raw[g], f"w1_{g}") for g in range(passes)]
+        def quantise(codes, plane, interleaved):
+            nc.vector.quantize_mx(out=codes.bitcast(FP8X4), scales=plane, in_=interleaved)
+
+        def round_weight(dealt, raw):
+            nc.vector.tensor_copy(
+                out=dealt.rearrange("p (u e) m j -> p m u j e", e=2),
+                in_=raw.rearrange("p j (m u e) -> p m u j e", u=2, e=2),
+            )
+
+        def quantise_weight_tiles(codes, plane, dealt, t0, t1):
+            cols = slice(t0 * P, t1 * P)
+            quantise(codes[:, cols], plane[:, cols], dealt[:, t0:t1].rearrange("p t m j -> p (t m j)"))
+
+        w1_codes, w1_planes = [], []
+        for g in range(PASSES):
+            dealt = held([P, PACK, P, PACK], BF16, f"w1_dealt{g}")
+            round_weight(dealt[:], w1_raw[g])
+            w1_codes.append(held([P, H], U32, f"w1_codes{g}"))
+            w1_planes.append(held([P, H], U8, f"w1_plane{g}"))
+            for t0 in (0, 2):
+                quantise_weight_tiles(w1_codes[g], w1_planes[g], dealt, t0, t0 + 2)
 
         banks = [psum.tile([P, BANK], F32, name=f"bank{b}") for b in range(8)]
         h = [held([P, T], F32, f"h{t}") for t in range(PACK)]
-        def hidden(t, use, halves=(0, 1)):
-            m_cols = slice(t * P, (t + 1) * P)
-            for half in halves:
-                cols = slice(half * BANK, (half + 1) * BANK)
-                acc = banks[use[half]]
-                for g in range(passes):
-                    nc.tensor.matmul_mx(
-                        out=acc[:],
-                        lhsT=w1_q[g][0][:, m_cols].bitcast(FP8X4),
-                        lhsT_scale=w1_q[g][1][:, m_cols],
-                        rhs=x_codes[half][:, g, :].bitcast(FP8X4),
-                        rhs_scale=x_plane[4 * g : P, cols],
-                        start=(g == 0),
-                        stop=(g == passes - 1),
-                    )
-                nc.scalar.activation(h[t][:, cols], acc[:], SILU)
-
-        w3_bf = held([P, PACK, P, PACK], BF16, "w3_bf")
+        w3_dealt = held([P, PACK, P, PACK], BF16, "w3_dealt")
         w3_codes = held([P, H], U32, "w3_codes")
         w3_plane = held([P, H], U8, "w3_plane")
 
-        def cast_w3(m0, m1, on_vector):
-            half = m0 // (P // 2)
-            src = w3_raw[half][:].rearrange("p j (m t) -> p m t j", t=PACK)[:, m0 - half * P // 2 : m1 - half * P // 2]
-            dst = w3_bf[:, :, m0:m1, :].rearrange("p t m j -> p m t j")
-            if on_vector:
-                nc.vector.tensor_copy(out=dst, in_=src)
-            else:
-                nc.scalar.copy(out=dst, in_=src)
+        def in_room(name, width):
+            first = room_at[QUANTISED_BEFORE_GATHER[name]]
+            return arena[:, first : first + width * PACK // 2].bitcast(BF16).rearrange("p (c j) -> p c j", j=PACK)
 
-        def quantise_w3(t0, t1):
-            cols = slice(t0 * P, t1 * P)
-            nc.vector.quantize_mx(out=w3_codes[:, cols].bitcast(FP8X4), scales=w3_plane[:, cols], in_=w3_bf[:, t0:t1].rearrange("p t m j -> p (t m j)"))
+        a_rounded = [held([P, PIECES[0][2], PACK], BF16, "a_rounded0")[:]]
+        a_rounded.extend(in_room(f"a{n}", PIECES[n][2]) for n in range(1, len(PIECES)))
 
-        def rows(start, pitch, count, width):
-            return arena[:, start : start + count * pitch].rearrange("p (t c) -> p t c", t=count)[:, :, :width]
-
-        def f_rows(n, t0, count):
-            k, width = PACK * n + t0, pieces[n][1]
-            pitch = f_at[k + 1] - f_at[k] if count > 1 else width
-            return rows(f_at[k], pitch, count, width)
-
-        def product(n, t):
-            start = product_at[PACK * n + t]
-            return arena[:, start : start + pieces[n][1]]
-
-        def interleaved(name, width):
-            if name in GUEST:
-                host, t, gw = GUEST[name]
-                start = room_at[PACK * host + t]
-                return arena[:, start : start + width * PACK // 2].bitcast(BF16).rearrange("p (c j) -> p c j", j=PACK)
-            return held([P, width, PACK], BF16, name)[:]
-
-        a_bf = [interleaved(f"a{n}", pieces[n][1]).rearrange("p (d c) j -> p d c j", d=1) for n in range(len(pieces))]
-
-        def cast_angles(n, c0, c1, on_vector):
-            dst = a_bf[n][:, :, c0:c1, :].rearrange("p d (c i) j -> p d c j i", i=4)
-            src = a_raw[n][:, :, :, c0:c1].rearrange("p j d (c i) -> p d c j i", i=4)
-            if on_vector:
-                nc.vector.tensor_copy(out=dst, in_=src)
-            else:
-                nc.scalar.copy(out=dst, in_=src)
+        def round_angles(copy, n, c0, c1):
+            copy(
+                out=a_rounded[n][:, c0:c1, :].rearrange("p (c i) j -> p c j i", i=4),
+                in_=a_raw[n][:, :, c0:c1].rearrange("p j (c i) -> p c j i", i=4),
+            )
 
         def quantise_angles(n):
-            v0, width, d0, nd = pieces[n]
-            codes = held([P, nd * width], U32, f"a_codes{n}")
-            plane = held([P, nd * width], U8, f"a_plane{n}")
-            nc.vector.quantize_mx(out=codes[:].bitcast(FP8X4), scales=plane[:], in_=a_bf[n].rearrange("p d c j -> p (d c j)"))
+            codes = held([P, PIECES[n][2]], U32, f"a_codes{n}")
+            plane = held([P, PIECES[n][2]], U8, f"a_plane{n}")
+            quantise(codes[:], plane[:], a_rounded[n].rearrange("p c j -> p (c j)"))
             return codes, plane
 
-        def filters(n, quantised, per_bank, use):
-            v0, width, d0, nd = pieces[n]
+        def multiply(acc, stationary, stationary_plane, moving, moving_plane, opens=True, closes=True):
+            nc.tensor.matmul_mx(
+                out=acc, lhsT=stationary, lhsT_scale=stationary_plane, rhs=moving.bitcast(FP8X4), rhs_scale=moving_plane, start=opens, stop=closes
+            )
+
+        def hidden(t, use):
+            m_cols = slice(t * P, (t + 1) * P)
+            for half in range(2):
+                cols = slice(half * BANK, (half + 1) * BANK)
+                acc = banks[use[half]][:]
+                for g in range(PASSES):
+                    multiply(
+                        acc, w1_codes[g][:, m_cols].bitcast(FP8X4), w1_planes[g][:, m_cols],
+                        x_codes[half][:, g, :], x_plane[4 * g : P, cols], g == 0, g == PASSES - 1,
+                    )
+                nc.scalar.activation(h[t][:, cols], acc, SILU)
+
+        def arena_rows(first, pitch, count, width):
+            return arena[:, first : first + count * pitch].rearrange("p (t c) -> p t c", t=count)[:, :, :width]
+
+        def filter_rows(n, t0, count):
+            k, width = PACK * n + t0, PIECES[n][2]
+            pitch = filter_at[k + 1] - filter_at[k] if count > 1 else width
+            return arena_rows(filter_at[k], pitch, count, width)
+
+        def filters(n, quantised, use):
             codes, plane = quantised
+            width, per_bank = PIECES[n][2], PACK // len(use)
             for t0 in range(0, PACK, per_bank):
                 acc = banks[use[t0 // per_bank]][:, : per_bank * width].rearrange("p (t c) -> p t c", t=per_bank)
                 for t in range(t0, t0 + per_bank):
                     m_cols = slice(t * P, (t + 1) * P)
-                    nc.tensor.matmul_mx(
-                        out=acc[:, t - t0, :],
-                        lhsT=w3_codes[:, m_cols].bitcast(FP8X4),
-                        lhsT_scale=w3_plane[:, m_cols],
-                        rhs=codes[:].bitcast(FP8X4),
-                        rhs_scale=plane[:],
-                        start=True,
-                        stop=True,
-                    )
-                nc.scalar.copy(out=f_rows(n, t0, per_bank), in_=acc)
+                    multiply(acc[:, t - t0, :], w3_codes[:, m_cols].bitcast(FP8X4), w3_plane[:, m_cols], codes[:], plane[:])
+                nc.scalar.copy(out=filter_rows(n, t0, per_bank), in_=acc)
+
+        def product(n, t):
+            first = product_at[PACK * n + t]
+            return arena[:, first : first + PIECES[n][2]]
 
         def messages(n):
-            v0, width, d, nd = pieces[n]
+            d, v0, width = PIECES[n]
             for t in range(PACK):
-                window = h[t][:].indirect(lists[d][:, v0 // 16 : (v0 + width) // 16])
-                nc.vector.tensor_tensor(product(n, t), window, f_rows(n, t, 1)[:, 0, :], MULT)
+                gathered = h[t][:].indirect(lists[d][:, v0 // PER_COLUMN : (v0 + width) // PER_COLUMN])
+                nc.vector.tensor_tensor(product(n, t), gathered, filter_rows(n, t, 1)[:, 0, :], MULT)
 
-        def piece_of(d, v0):
-            return [n for n, (p0, pw, pd, nd) in enumerate(pieces) if pd == d and p0 <= v0 < p0 + pw][0]
+        def piece_of(d, v):
+            return [n for n, (pd, v0, width) in enumerate(PIECES) if pd == d and v0 <= v < v0 + width][0]
 
-        def add_on_vector(v0, width, z):
-            both = []
+        def sum_on_vector(v0, z_part):
+            terms = []
             for d in range(D):
                 n = piece_of(d, v0)
                 k = PACK * n
-                assert product_at[k + 2] - product_at[k + 1] == product_at[k + 1] - product_at[k] == product_at[k + 3] - product_at[k + 2]
-                view = rows(product_at[k] + v0 - pieces[n][0], product_at[k + 1] - product_at[k], PACK, width)
-                both.append(view.rearrange("p t (c i) -> p c t i", i=2))
-            nc.vector.tensor_tensor(z.rearrange("p (c i) t -> p c t i", i=2), both[0], both[1], ADD)
+                view = arena_rows(product_at[k] + v0 - PIECES[n][1], product_at[k + 1] - product_at[k], PACK, P)
+                terms.append(view.rearrange("p t (c i) -> p c t i", i=2))
+            nc.vector.tensor_tensor(z_part.rearrange("p (c i) t -> p c t i", i=2), terms[0], terms[1], ADD)
 
-        def turn(blocks):
+        def sum_on_tensor(blocks):
             for t in range(PACK):
                 for v0, bank in blocks:
                     for d in reversed(range(D)):
                         n = piece_of(d, v0)
-                        c0 = v0 - pieces[n][0]
-                        nc.tensor.matmul(banks[bank][:, t * P : (t + 1) * P], lhsT=product(n, t)[:, c0 : c0 + P], rhs=ident[:], start=(d == D - 1), stop=(d == 0), is_transpose=True)
+                        c0 = v0 - PIECES[n][1]
+                        nc.tensor.matmul(
+                            banks[bank][:, t * P : (t + 1) * P], lhsT=product(n, t)[:, c0 : c0 + P], rhs=ident[:],
+                            start=(d == D - 1), stop=(d == 0), is_transpose=True,
+                        )
 
         def round_sums(v0, bank):
             rounded = held([P, 2, P, 2], BF16, f"rounded{v0}")
             nc.scalar.copy(out=rounded[:], in_=banks[bank][:].rearrange("v (u e p) -> v u p e", u=2, e=2))
             return rounded
 
-        def warm_up(bank, count):
-            codes, plane = w1_q[0]
-            for i in range(count):
-                nc.tensor.matmul_mx(out=banks[bank][:], lhsT=codes[:, :P].bitcast(FP8X4), lhsT_scale=plane[:, :P], rhs=codes[:].bitcast(FP8X4), rhs_scale=plane[:], start=True, stop=True)
-
-        def turn_back(roundeds, bank, z):
-            back = banks[bank][:, : len(roundeds) * 2 * P].rearrange("p (b u v) -> p b u v", u=2, v=P)
-            for b, rounded in enumerate(roundeds):
+        def turn_back(blocks, bank, z_part):
+            back = banks[bank][:].rearrange("p (b u v) -> p b u v", u=2, v=P)
+            for b, rounded in enumerate(blocks):
                 words = rounded[:].rearrange("v u p e -> v (u p e)").bitcast(F32)
                 for u in range(2):
                     nc.tensor.transpose(back[:, b, u, :], words[:, u * P : (u + 1) * P], ident[:])
-            z_words = z.rearrange("p c t -> p (c t)").bitcast(F32).rearrange("p (b v u) -> p b v u", u=2, v=P)
+            z_words = z_part.rearrange("p c t -> p (c t)").bitcast(F32).rearrange("p (b v u) -> p b v u", u=2, v=P)
             nc.scalar.copy(out=z_words, in_=back.rearrange("p b u v -> p b v u"))
 
-        def project(v0, width, z, bank):
+        def project(v0, z_part, bank):
+            width = z_part.shape[1]
             codes = held([P, width], U32, f"z_codes{v0}")
             plane = held([P, width], U8, f"z_plane{v0}")
-            nc.vector.quantize_mx(out=codes[:].bitcast(FP8X4), scales=plane[:], in_=z.rearrange("p c t -> p (c t)"))
+            quantise(codes[:], plane[:], z_part.rearrange("p c t -> p (c t)"))
             acc = banks[bank][:, :width]
-            nc.tensor.matmul_mx(
-                out=acc[:],
-                lhsT=w2_codes[:].bitcast(FP4X4),
-                lhsT_scale=w2_plane[:],
-                rhs=codes[:].bitcast(FP8X4),
-                rhs_scale=plane[:],
-                start=True,
-                stop=True,
-            )
-            res = held([P, width], F32, f"res{v0}")
-            nc.scalar.copy(out=res[:], in_=acc[:])
-            nc.sync.dma_start(out=out[:, v0 : v0 + width], in_=res[:])
+            multiply(acc, w2_codes[:].bitcast(FP4X4), w2_plane[:], codes[:], plane[:])
+            result = held([P, width], F32, f"result{v0}")
+            nc.scalar.copy(out=result[:], in_=acc)
+            nc.sync.dma_start(out=out[:, v0 : v0 + width], in_=result[:])
 
-        z = {v0: interleaved(f"z{v0}", width) for v0, width in ((0, 256), (256, 256), (512, 256))}
-        z[768] = z[512][:, :128, :]
-        z[896] = z[512][:, 128:, :]
-        warm_up(7, 3)
+        z0, z256 = in_room("z0", Z_WIDTH), in_room("z256", Z_WIDTH)
+        z512 = held([P, Z_WIDTH, PACK], BF16, "z512")[:]
+        z768, z896 = z512[:, :P, :], z512[:, P:, :]
+        on_vector, on_scalar = nc.vector.tensor_copy, nc.scalar.copy
+
+        for repeat in range(WARM_PASSES):
+            multiply(banks[7][:], w1_codes[0][:, :P].bitcast(FP8X4), w1_planes[0][:, :P], w1_codes[0][:], w1_planes[0][:])
+
         hidden(0, (0, 1))
         hidden(1, (2, 3))
-        cast_angles(0, 0, 256, True)
-        q0 = quantise_angles(0)
-        cast_w3(0, 64, True)
-        cast_w3(64, 128, True)
-        quantise_w3(0, 1)
-        quantise_w3(1, 2)
-        quantise_w3(2, 4)
-        filters(0, q0, 1, (4, 5, 6, 7))
+        round_angles(on_vector, 0, 0, PIECES[0][2])
+        quantised0 = quantise_angles(0)
+        for half in range(2):
+            round_weight(w3_dealt[:, :, half * P // 2 : (half + 1) * P // 2, :], w3_raw[half])
+        for t0, t1 in ((0, 1), (1, 2), (2, 4)):
+            quantise_weight_tiles(w3_codes, w3_plane, w3_dealt, t0, t1)
+        filters(0, quantised0, (4, 5, 6, 7))
         hidden(2, (0, 1))
         hidden(3, (2, 3))
-        cast_angles(1, 0, 256, True)
-        filters(1, quantise_angles(1), 2, (0, 1))
-        cast_angles(2, 0, 256, False)
+
+        round_angles(on_vector, 1, 0, PIECES[1][2])
+        filters(1, quantise_angles(1), (0, 1))
+        round_angles(on_scalar, 2, 0, SCALAR_SHARE)
         messages(0)
-        cast_angles(2, 256, 512, True)
-        cast_angles(3, 0, 512, False)
-        filters(2, quantise_angles(2), 1, (2, 3, 4, 5))
+        round_angles(on_vector, 2, SCALAR_SHARE, PIECES[2][2])
+        round_angles(on_scalar, 3, 0, PIECES[3][2])
+        filters(2, quantise_angles(2), (2, 3, 4, 5))
         messages(1)
-        filters(3, quantise_angles(3), 1, (6, 7, 4, 5))
+        filters(3, quantise_angles(3), (6, 7, 4, 5))
         messages(2)
-        cast_angles(4, 0, 256, False)
-        q4 = quantise_angles(4)
-        cast_angles(5, 0, 256, False)
-        q5 = quantise_angles(5)
-        turn([(0, 0), (128, 1), (256, 2), (384, 3)])
-        r = [round_sums(128 * b, b) for b in range(4)]
-        filters(4, q4, 2, (6, 7))
-        turn_back(r[:2], 0, z[0])
-        turn_back(r[2:], 2, z[256])
-        filters(5, q5, 2, (4, 5))
+        round_angles(on_scalar, 4, 0, PIECES[4][2])
+        quantised4 = quantise_angles(4)
+        round_angles(on_scalar, 5, 0, PIECES[5][2])
+        quantised5 = quantise_angles(5)
+
+        sum_on_tensor([(P * b, b) for b in range(4)])
+        rounded_blocks = [round_sums(P * b, b) for b in range(4)]
+        filters(4, quantised4, (6, 7))
+        turn_back(rounded_blocks[:2], 0, z0)
+        turn_back(rounded_blocks[2:], 2, z256)
+        filters(5, quantised5, (4, 5))
         messages(3)
-        project(0, 256, z[0], 1)
+        project(0, z0, 1)
         messages(4)
-        turn([(512, 2), (640, 3)])
-        r = [round_sums(512, 2), round_sums(640, 3)]
-        turn_back(r, 6, z[512])
-        project(256, 256, z[256], 6)
+
+        sum_on_tensor([(512, 2), (640, 3)])
+        turn_back([round_sums(512, 2), round_sums(640, 3)], 6, z512)
+        project(256, z256, 6)
         messages(5)
-        project(512, 256, z[512], 7)
-        add_on_vector(768, 128, z[768])
-        add_on_vector(896, 128, z[896])
-        project(768, 128, z[768], 4)
-        project(896, 128, z[896], 5)
+        project(512, z512, 7)
+
+        sum_on_vector(768, z768)
+        sum_on_vector(896, z896)
+        project(768, z768, 4)
+        project(896, z896, 5)

from contextlib import ExitStack

import concourse.mybir as mybir
from concourse.masks import make_identity

K, T, H, N, J, D = 1024, 1024, 512, 128, 512, 2
FLOPS = 2 * (K * H * T + J * H * D * T + H * N * T)

F32 = mybir.dt.float32
BF16 = mybir.dt.bfloat16
I32 = mybir.dt.int32
U32 = mybir.dt.uint32
U16 = mybir.dt.uint16
U8 = mybir.dt.uint8
FP8X4 = mybir.dt.float8_e4m3fn_x4
FP4X4 = mybir.dt.float4_e2m1fn_x4
SILU = mybir.ActivationFunctionType.Silu
MULT = mybir.AluOpType.mult
ADD = mybir.AluOpType.add

P = 128
PACK = 4
PASSES = K // (P * PACK)
BANK = 512
QUADRANT = 32
PER_COLUMN = 16
Z_WIDTH = 256
WARM_PASSES = 3

PIECES = [(0, 0, 256), (0, 256, 256), (1, 0, 512), (0, 512, 512), (1, 512, 256), (1, 768, 256)]
SUMMED_ON_VECTOR = (3, 5)
SCALAR_SHARE = 320

QUANTISED_BEFORE_GATHER = {"a1": 2, "a2": 6, "a3": 8, "a4": 12, "a5": 14, "z0": 18, "z256": 20}
MIN_LAP = 64


def arena_layout():
    gathers = PACK * len(PIECES)
    guest_words = {}
    for name, k in QUANTISED_BEFORE_GATHER.items():
        columns = PIECES[int(name[1:])][2] if name.startswith("a") else Z_WIDTH
        guest_words.setdefault(k, columns * PACK // 2)
    filter_at, product_at, room_at, end = {}, {}, {}, 0
    for k in range(0, gathers, 2):
        n = k // PACK
        width = PIECES[n][2]
        old_width = PIECES[max(k - 2, 0) // PACK][2]
        pairs = (PACK * n, PACK * n + 2) if n in SUMMED_ON_VECTOR else (k,)
        room = max([2 * (width - old_width)] + [guest_words.get(pair, 0) for pair in pairs])
        lap = max(min(old_width, width - room // 4), MIN_LAP)
        filter_at[k - 2] = end
        room_at[k] = end + old_width
        filter_at[k - 1] = room_at[k] + room
        product_at[k] = room_at[k] - lap
        product_at[k + 1] = filter_at[k - 1] + lap - width
        end = filter_at[k - 1] + old_width
    last_width = PIECES[-1][2]
    filter_at[gathers - 2] = end
    filter_at[gathers - 1] = end + last_width
    return filter_at, product_at, room_at, end + 2 * last_width


def tile_picked_wdime_none_l_kernel(tc, x_words, x_scales, aT, w1, w3, w2_words, w2_scales, pos1, pos2, out):
    nc = tc.nc
    filter_at, product_at, room_at, arena_words = arena_layout()

    with ExitStack() as ctx:
        keep = ctx.enter_context(tc.tile_pool(name="keep", bufs=1))
        psum = ctx.enter_context(tc.psum_pool(name="psum", bufs=1))

        def held(shape, dtype, name):
            return keep.tile(shape, dtype, name=name, align_bytes=64)

        x_plane = held([P, T], U8, "x_plane")
        nc.gpsimd.memset(x_plane[:].bitcast(I32), 0)
        w2_plane = held([P, N], U8, "w2_plane")
        nc.vector.memset(w2_plane[:].bitcast(I32), 0)
        ident = held([P, P], F32, "ident")
        make_identity(nc, ident[:])
        arena = held([P, arena_words], F32, "arena")

        def load_rows(rows, name):
            raw = held([P, PACK, rows.shape[1]], F32, name)
            nc.sync.dma_start(out=raw[:], in_=rows.rearrange("(p j) c -> p j c", j=PACK))
            return raw[:]

        def piece_columns(n):
            d, v0, width = PIECES[n]
            return aT[:, d * T + v0 : d * T + v0 + width]

        def load_x_scales(g):
            by_row = x_scales[g].rearrange("(q r) c -> r q c", r=4)
            for r in range(4):
                nc.sync.dma_start(out=x_plane[4 * g + r : P : QUADRANT, :].bitcast(I32), in_=by_row[r].bitcast(I32))

        def load_x_codes(half):
            codes = held([P, PASSES, BANK], U32, f"x_codes{half}")
            byte_rows = x_words.rearrange("g p n r -> p g (n r)")
            nc.sync.dma_start(out=codes[:].bitcast(I32), in_=byte_rows[:, :, half * BANK * PACK : (half + 1) * BANK * PACK].bitcast(I32))
            return codes

        def load_list(name, pos):
            offsets = keep.tile([P, T // PER_COLUMN], U16, name=name)
            nc.sync.dma_start(offsets[:], pos)
            return offsets

        w1_raw = [load_rows(w1[: P * PACK, :], "w1_raw0")]
        load_x_scales(0)
        w1_raw.append(load_rows(w1[P * PACK :, :], "w1_raw1"))
        x_codes = [load_x_codes(0)]
        load_x_scales(1)
        x_codes.append(load_x_codes(1))
        a_raw = [load_rows(piece_columns(0), "a_raw0")]
        w3_raw = [load_rows(w3[:, half * H // 2 : (half + 1) * H // 2], f"w3_raw{half}") for half in range(2)]
        lists = [load_list("pos1", pos1)]
        a_raw.extend(load_rows(piece_columns(n), f"a_raw{n}") for n in (1, 2))
        lists.append(load_list("pos2", pos2))
        raw_at = filter_at[PACK * 2] + PIECES[2][2] // 2
        piece3_raw = arena[:, raw_at : raw_at + PACK * PIECES[3][2]].rearrange("p (j c) -> p j c", j=PACK)
        nc.sync.dma_start(out=piece3_raw, in_=piece_columns(3).rearrange("(p j) c -> p j c", j=PACK))
        a_raw.append(piece3_raw)
        a_raw.extend(load_rows(piece_columns(n), f"a_raw{n}") for n in (4, 5))
        w2_codes = held([P, 2 * N], U8, "w2_codes")
        nc.sync.dma_start(out=w2_codes[:].bitcast(I32), in_=w2_words[0].bitcast(I32))
        for q in range(4):
            nc.sync.dma_start(
                out=w2_plane[QUADRANT * q : QUADRANT * q + 4, :].bitcast(I32),
                in_=w2_scales[0, 4 * q : 4 * q + 4, :].bitcast(I32),
            )

        def quantise(codes, plane, interleaved):
            nc.vector.quantize_mx(out=codes.bitcast(FP8X4), scales=plane, in_=interleaved)

        def round_weight(dealt, raw):
            nc.vector.tensor_copy(
                out=dealt.rearrange("p (u e) m j -> p m u j e", e=2),
                in_=raw.rearrange("p j (m u e) -> p m u j e", u=2, e=2),
            )

        def quantise_weight_tiles(codes, plane, dealt, t0, t1):
            cols = slice(t0 * P, t1 * P)
            quantise(codes[:, cols], plane[:, cols], dealt[:, t0:t1].rearrange("p t m j -> p (t m j)"))

        w1_codes, w1_planes = [], []
        for g in range(PASSES):
            dealt = held([P, PACK, P, PACK], BF16, f"w1_dealt{g}")
            round_weight(dealt[:], w1_raw[g])
            w1_codes.append(held([P, H], U32, f"w1_codes{g}"))
            w1_planes.append(held([P, H], U8, f"w1_plane{g}"))
            for t0 in (0, 2):
                quantise_weight_tiles(w1_codes[g], w1_planes[g], dealt, t0, t0 + 2)

        banks = [psum.tile([P, BANK], F32, name=f"bank{b}") for b in range(8)]
        h = [held([P, T], F32, f"h{t}") for t in range(PACK)]
        w3_dealt = held([P, PACK, P, PACK], BF16, "w3_dealt")
        w3_codes = held([P, H], U32, "w3_codes")
        w3_plane = held([P, H], U8, "w3_plane")

        def in_room(name, width):
            first = room_at[QUANTISED_BEFORE_GATHER[name]]
            return arena[:, first : first + width * PACK // 2].bitcast(BF16).rearrange("p (c j) -> p c j", j=PACK)

        a_rounded = [held([P, PIECES[0][2], PACK], BF16, "a_rounded0")[:]]
        a_rounded.extend(in_room(f"a{n}", PIECES[n][2]) for n in range(1, len(PIECES)))

        def round_angles(copy, n, c0, c1):
            copy(
                out=a_rounded[n][:, c0:c1, :].rearrange("p (c i) j -> p c j i", i=4),
                in_=a_raw[n][:, :, c0:c1].rearrange("p j (c i) -> p c j i", i=4),
            )

        def quantise_angles(n):
            codes = held([P, PIECES[n][2]], U32, f"a_codes{n}")
            plane = held([P, PIECES[n][2]], U8, f"a_plane{n}")
            quantise(codes[:], plane[:], a_rounded[n].rearrange("p c j -> p (c j)"))
            return codes, plane

        def multiply(acc, stationary, stationary_plane, moving, moving_plane, opens=True, closes=True):
            nc.tensor.matmul_mx(
                out=acc, lhsT=stationary, lhsT_scale=stationary_plane, rhs=moving.bitcast(FP8X4), rhs_scale=moving_plane, start=opens, stop=closes
            )

        def hidden(t, use):
            m_cols = slice(t * P, (t + 1) * P)
            for half in range(2):
                cols = slice(half * BANK, (half + 1) * BANK)
                acc = banks[use[half]][:]
                for g in range(PASSES):
                    multiply(
                        acc, w1_codes[g][:, m_cols].bitcast(FP8X4), w1_planes[g][:, m_cols],
                        x_codes[half][:, g, :], x_plane[4 * g : P, cols], g == 0, g == PASSES - 1,
                    )
                nc.scalar.activation(h[t][:, cols], acc, SILU)

        def arena_rows(first, pitch, count, width):
            return arena[:, first : first + count * pitch].rearrange("p (t c) -> p t c", t=count)[:, :, :width]

        def filter_rows(n, t0, count):
            k, width = PACK * n + t0, PIECES[n][2]
            pitch = filter_at[k + 1] - filter_at[k] if count > 1 else width
            return arena_rows(filter_at[k], pitch, count, width)

        def filters(n, quantised, use):
            codes, plane = quantised
            width, per_bank = PIECES[n][2], PACK // len(use)
            for t0 in range(0, PACK, per_bank):
                acc = banks[use[t0 // per_bank]][:, : per_bank * width].rearrange("p (t c) -> p t c", t=per_bank)
                for t in range(t0, t0 + per_bank):
                    m_cols = slice(t * P, (t + 1) * P)
                    multiply(acc[:, t - t0, :], w3_codes[:, m_cols].bitcast(FP8X4), w3_plane[:, m_cols], codes[:], plane[:])
                nc.scalar.copy(out=filter_rows(n, t0, per_bank), in_=acc)

        def product(n, t):
            first = product_at[PACK * n + t]
            return arena[:, first : first + PIECES[n][2]]

        def messages(n):
            d, v0, width = PIECES[n]
            for t in range(PACK):
                gathered = h[t][:].indirect(lists[d][:, v0 // PER_COLUMN : (v0 + width) // PER_COLUMN])
                nc.vector.tensor_tensor(product(n, t), gathered, filter_rows(n, t, 1)[:, 0, :], MULT)

        def piece_of(d, v):
            return [n for n, (pd, v0, width) in enumerate(PIECES) if pd == d and v0 <= v < v0 + width][0]

        def sum_on_vector(v0, z_part):
            terms = []
            for d in range(D):
                n = piece_of(d, v0)
                k = PACK * n
                view = arena_rows(product_at[k] + v0 - PIECES[n][1], product_at[k + 1] - product_at[k], PACK, P)
                terms.append(view.rearrange("p t (c i) -> p c t i", i=2))
            nc.vector.tensor_tensor(z_part.rearrange("p (c i) t -> p c t i", i=2), terms[0], terms[1], ADD)

        def sum_on_tensor(blocks):
            for t in range(PACK):
                for v0, bank in blocks:
                    for d in reversed(range(D)):
                        n = piece_of(d, v0)
                        c0 = v0 - PIECES[n][1]
                        nc.tensor.matmul(
                            banks[bank][:, t * P : (t + 1) * P], lhsT=product(n, t)[:, c0 : c0 + P], rhs=ident[:],
                            start=(d == D - 1), stop=(d == 0), is_transpose=True,
                        )

        def round_sums(v0, bank):
            rounded = held([P, 2, P, 2], BF16, f"rounded{v0}")
            nc.scalar.copy(out=rounded[:], in_=banks[bank][:].rearrange("v (u e p) -> v u p e", u=2, e=2))
            return rounded

        def turn_back(blocks, bank, z_part):
            back = banks[bank][:].rearrange("p (b u v) -> p b u v", u=2, v=P)
            for b, rounded in enumerate(blocks):
                words = rounded[:].rearrange("v u p e -> v (u p e)").bitcast(F32)
                for u in range(2):
                    nc.tensor.transpose(back[:, b, u, :], words[:, u * P : (u + 1) * P], ident[:])
            z_words = z_part.rearrange("p c t -> p (c t)").bitcast(F32).rearrange("p (b v u) -> p b v u", u=2, v=P)
            nc.scalar.copy(out=z_words, in_=back.rearrange("p b u v -> p b v u"))

        def project(v0, z_part, bank):
            width = z_part.shape[1]
            codes = held([P, width], U32, f"z_codes{v0}")
            plane = held([P, width], U8, f"z_plane{v0}")
            quantise(codes[:], plane[:], z_part.rearrange("p c t -> p (c t)"))
            acc = banks[bank][:, :width]
            multiply(acc, w2_codes[:].bitcast(FP4X4), w2_plane[:], codes[:], plane[:])
            result = held([P, width], F32, f"result{v0}")
            nc.scalar.copy(out=result[:], in_=acc)
            nc.sync.dma_start(out=out[:, v0 : v0 + width], in_=result[:])

        z0, z256 = in_room("z0", Z_WIDTH), in_room("z256", Z_WIDTH)
        z512 = held([P, Z_WIDTH, PACK], BF16, "z512")[:]
        z768, z896 = z512[:, :P, :], z512[:, P:, :]
        on_vector, on_scalar = nc.vector.tensor_copy, nc.scalar.copy

        for repeat in range(WARM_PASSES):
            multiply(banks[7][:], w1_codes[0][:, :P].bitcast(FP8X4), w1_planes[0][:, :P], w1_codes[0][:], w1_planes[0][:])

        hidden(0, (0, 1))
        hidden(1, (2, 3))
        round_angles(on_vector, 0, 0, PIECES[0][2])
        quantised0 = quantise_angles(0)
        for half in range(2):
            round_weight(w3_dealt[:, :, half * P // 2 : (half + 1) * P // 2, :], w3_raw[half])
        for t0, t1 in ((0, 1), (1, 2), (2, 4)):
            quantise_weight_tiles(w3_codes, w3_plane, w3_dealt, t0, t1)
        filters(0, quantised0, (4, 5, 6, 7))
        hidden(2, (0, 1))
        hidden(3, (2, 3))

        round_angles(on_vector, 1, 0, PIECES[1][2])
        filters(1, quantise_angles(1), (0, 1))
        round_angles(on_scalar, 2, 0, SCALAR_SHARE)
        messages(0)
        round_angles(on_vector, 2, SCALAR_SHARE, PIECES[2][2])
        round_angles(on_scalar, 3, 0, PIECES[3][2])
        filters(2, quantise_angles(2), (2, 3, 4, 5))
        messages(1)
        filters(3, quantise_angles(3), (6, 7, 4, 5))
        messages(2)
        round_angles(on_scalar, 4, 0, PIECES[4][2])
        quantised4 = quantise_angles(4)
        round_angles(on_scalar, 5, 0, PIECES[5][2])
        quantised5 = quantise_angles(5)

        sum_on_tensor([(P * b, b) for b in range(4)])
        rounded_blocks = [round_sums(P * b, b) for b in range(4)]
        filters(4, quantised4, (6, 7))
        turn_back(rounded_blocks[:2], 0, z0)
        turn_back(rounded_blocks[2:], 2, z256)
        filters(5, quantised5, (4, 5))
        messages(3)
        project(0, z0, 1)
        messages(4)

        sum_on_tensor([(512, 2), (640, 3)])
        turn_back([round_sums(512, 2), round_sums(640, 3)], 6, z512)
        project(256, z256, 6)
        messages(5)
        project(512, z512, 7)

        sum_on_vector(768, z768)
        sum_on_vector(896, z896)
        project(768, z768, 4)
        project(896, z896, 5)
